import numpy as np
import ml_dtypes


def mxq(x, axis, fmt="e4m3"):
    dtype, down = {"e4m3": (ml_dtypes.float8_e4m3fn, 7), "e5m2": (ml_dtypes.float8_e5m2, 14)}[fmt]
    v = np.moveaxis(np.asarray(x, np.float32).astype(ml_dtypes.bfloat16).astype(np.float64), axis, -1)
    blocks = v.reshape(v.shape[:-1] + (-1, 32))
    amax = np.abs(blocks).max(-1, keepdims=True)
    byte = np.maximum(np.where(amax > 0, np.frexp(amax)[1] - 1 + 127, 0) - down, 1)
    scale = np.exp2(byte - 127.0)
    codes = (blocks / scale).astype(np.float32).astype(dtype).astype(np.float64)
    return np.moveaxis((codes * scale).reshape(v.shape), -1, axis)


WIDE = False


def mx_kscale(k):
    if not WIDE:
        return np.ones(k)
    levels = np.array([10, -10, 5, -5, 0])
    if k % 512:
        return np.exp2(np.random.permutation(np.resize(levels, k // 32))).repeat(32)
    a = np.empty((k // 512, 16))
    for p in range(k // 512):
        a[p, :8] = np.random.permutation(np.resize(levels, 8))
        for g in range(8):
            far = levels[np.abs(levels - a[p, g]) >= 10]
            a[p, g + 8] = far[np.random.randint(len(far))]
    return np.exp2(a.ravel()).repeat(32)


def f64(x):
    return np.asarray(x).astype(np.float64)


def striped(idx):
    return np.tile(idx.reshape(-1, 16).T, (8, 1)).astype(np.uint16)


def unstriped(offs):
    return offs[:16].T.reshape(-1).astype(np.int64)


E2M1 = np.array([0.0, 0.5, 1.0, 1.5, 2.0, 3.0, 4.0, 6.0, -0.0, -0.5, -1.0, -1.5, -2.0, -3.0, -4.0, -6.0])


def pack_weight(w, fmt):
    k, n = w.shape
    w = f64(np.asarray(w, np.float32).astype(ml_dtypes.bfloat16)).reshape(k // 32, 32, n)
    amax = np.abs(w).max(1)
    if fmt == "e4m3":
        byte = np.frexp(amax)[1] - 1 + 127 - 7
    else:
        mant, ex = np.frexp(amax / 6.0)
        byte = np.where(mant > 0.5, ex, ex - 1) + 127
    byte = np.clip(np.where(amax > 0, byte, 1), 1, 254)
    scaled = (w * np.exp2(127.0 - byte)[:, None, :]).reshape(k, n).astype(np.float32)
    by_word = np.ascontiguousarray(scaled.reshape(k // 512, 128, 4, n).transpose(0, 1, 3, 2))
    if fmt == "e4m3":
        words = by_word.astype(ml_dtypes.float8_e4m3fn).view(np.uint8)
    else:
        c = by_word.astype(ml_dtypes.float4_e2m1fn).view(np.uint8) & 0xF
        words = (c[..., 0::2] | (c[..., 1::2] << 4)).reshape(k // 512, 128, 2 * n)
    return np.ascontiguousarray(words), np.ascontiguousarray(byte.astype(np.uint8).reshape(k // 512, 16, n))


def unpack_weight(words, scales, fmt):
    g, _, n = scales.shape
    words = np.ascontiguousarray(words).reshape(g, 128, n, -1)
    if fmt == "e4m3":
        vals = words.view(ml_dtypes.float8_e4m3fn).astype(np.float64)
    else:
        nib = np.empty((g, 128, n, 4), np.uint8)
        nib[..., 0::2] = words & 0xF
        nib[..., 1::2] = words >> 4
        vals = E2M1[nib]
    vals = vals * np.repeat(np.exp2(scales.astype(np.float64) - 127.0), 8, axis=1)[..., None]
    return vals.transpose(0, 1, 3, 2).reshape(g * 512, n)


def gelu(v):
    return 0.5 * v * (1.0 + np.tanh(np.sqrt(2.0 / np.pi) * (v + 0.044715 * v**3)))


K, T, S, H, T2, P = 1536, 2048, 1024, 512, 2048, 1024


def setup_inputs():
    n = np.random.standard_normal
    s = mx_kscale(K)[:, None]
    u = mx_kscale(H)[:, None]
    d = {}
    d["tab_words"], d["tab_scales"] = pack_weight(n((K, T)) * s, "e4m3")
    d["offs"] = striped(np.random.permutation(T)[:S])
    d["offs2"] = striped(np.random.permutation(T2)[:S])
    d["offs3"] = striped(np.random.permutation(T2)[:P])
    d["offs4"] = striped(np.random.permutation(T2)[:P])
    d["w1"] = (n((K, H)) / K**0.5 / s).astype(np.float32)
    d["gain"] = (np.exp(0.3 * n(H)) * u[:, 0]).astype(np.float32)
    d["wgs"] = np.exp(0.3 * n((128, S))).astype(np.float32)
    d["page0"] = (n((H, T2)) * u).astype(np.float32)
    d["wear"] = np.exp(0.3 * n(H)).astype(np.float32)
    d["w2_words"], d["w2_scales"] = pack_weight(1.3 * n((H, H)) / H**0.5 / u, "e2m1")
    d["lift"] = (np.exp(0.3 * n(H)) * u[:, 0]).astype(np.float32)
    d["w3"] = (1.4 * n((H, H)) / H**0.5 / u).astype(np.float32)
    d["w4_words"], d["w4_scales"] = pack_weight(1.4 * n((H, H)) / H**0.5 / u, "e4m3")
    d["octave"] = (np.exp(0.3 * n(H)) / u[:, 0]).astype(np.float32)
    return d


def reference(tab_words, tab_scales, offs, offs2, offs3, offs4, w1, gain, wgs, page0, wear,
              w2_words, w2_scales, lift, w3, w4_words, w4_scales, octave):
    v = unpack_weight(tab_words, tab_scales, "e4m3")[:, unstriped(offs)]
    h = f64(gain)[:, None] * (mxq(f64(w1), 0, "e4m3").T @ v)
    page = f64(page0).copy()
    page[:, unstriped(offs2)] = np.tile(f64(wgs), (H // 128, 1)) * h
    x = mxq(f64(wear)[:, None] * page[:, unstriped(offs3)], 0, "e4m3")
    w2 = unpack_weight(w2_words, w2_scales, "e2m1")
    g = mxq(f64(lift)[:, None] * np.tanh(w2.T @ x), 0, "e4m3")
    y = mxq(f64(w3), 0, "e4m3").T @ g
    y2 = unpack_weight(w4_words, w4_scales, "e4m3").T @ g
    keys = f64(octave)[:, None] * page[:, unstriped(offs4)]
    return y * keys + y2

@@ -1,0 +1,309 @@
+from contextlib import ExitStack
+
+import concourse.mybir as mybir
+
+K, T, S, H, T2, NP = 1536, 2048, 1024, 512, 2048, 1024
+FLOPS = 2 * (K * H * S + 3 * H * H * NP)
+
+F32 = mybir.dt.float32
+BF16 = mybir.dt.bfloat16
+I32 = mybir.dt.int32
+U32 = mybir.dt.uint32
+U16 = mybir.dt.uint16
+U8 = mybir.dt.uint8
+FP8X4 = mybir.dt.float8_e4m3fn_x4
+FP4X4 = mybir.dt.float4_e2m1fn_x4
+MULT = mybir.AluOpType.mult
+ADD = mybir.AluOpType.add
+COPY = mybir.ActivationFunctionType.Copy
+TANH = mybir.ActivationFunctionType.Tanh
+
+P = 128
+PACK = 4
+PASSES = K // (P * PACK)
+BANK = 512
+HALVES = S // BANK
+CHUNK = 256
+CHUNKS = NP // CHUNK
+QUADS = 4
+
+
+def tile_list_key_action_ledger_kernel(
+    tc, tab_words, tab_scales, offs, offs2, offs3, offs4, w1, gain, wgs, page0, wear,
+    w2_words, w2_scales, lift, w3, w4_words, w4_scales, octave, out,
+):
+    nc = tc.nc
+    with ExitStack() as ctx:
+        lists = ctx.enter_context(tc.tile_pool(name="lists", bufs=1))
+        keep = ctx.enter_context(tc.tile_pool(name="keep", bufs=1))
+        ring = ctx.enter_context(tc.tile_pool(name="ring", bufs=2))
+        psum = ctx.enter_context(tc.psum_pool(name="psum", bufs=1))
+
+        def load_list(name, source):
+            tile = lists.tile([P, S // 16], U16, name=name)
+            nc.sync.dma_start(tile[:], source)
+            return tile
+
+        def load_weight_rows(rows):
+            raw = keep.tile([P, PACK, H], F32, name="w_raw", bufs=PASSES)
+            nc.sync.dma_start(raw[:], rows.rearrange("(p j) c -> p j c", j=PACK))
+            return raw
+
+        def load_table_words(a):
+            words = keep.tile([P, T], U32, name="tab_w%d" % a)
+            nc.sync.dma_start(words[:].bitcast(I32), tab_words[a].rearrange("p t i -> p (t i)").bitcast(I32))
+            return words
+
+        def load_page(t):
+            page = keep.tile([P, T2], F32, name="page%d" % t)
+            nc.sync.dma_start(page[:], page0.rearrange("(p t) c -> p t c", t=PACK)[:, t, :])
+            return page
+
+        wgs_rows = wgs.rearrange("(q t) c -> q t c", t=PACK)
+
+        def load_wgs(name, ts, cols):
+            tile = keep.tile([P, ts.stop - ts.start, cols.stop - cols.start], F32, name=name)
+            for quad in (0, 2, 1, 3):
+                nc.sync.dma_start(tile[32 * quad : 32 * quad + 32, :, :], wgs_rows[:, ts, cols])
+            return tile
+
+        def load_vector(name, source):
+            tile = keep.tile([P, PACK], F32, name=name)
+            nc.gpsimd.dma_start(tile[:], source.rearrange("(p t) -> p t", t=PACK))
+            return tile
+
+        def quantize(name, grouped, width, tag=""):
+            codes = keep.tile([P, width], U32, name=name + "_codes", tag=tag, align_bytes=64)
+            scales = keep.tile([P, width], U8, name=name + "_scales", align_bytes=64)
+            nc.vector.quantize_mx(out=codes[:].bitcast(FP8X4), scales=scales[:], in_=grouped[:])
+            return codes, scales
+
+        def quantize_weight(name, raw, tag=""):
+            grouped = ring.tile([P, H * PACK], BF16, name="w_grouped", align_bytes=64)
+            nc.scalar.copy(
+                out=grouped[:].rearrange("p (t m j) -> p m j t", t=PACK, j=PACK),
+                in_=raw[:].rearrange("p j (m t) -> p m j t", t=PACK),
+            )
+            return quantize(name, grouped, H, tag)
+
+        def bank(b, shape):
+            return psum.tile(shape, F32, name="bank%d" % b)
+
+        tab_s = keep.tile([P, T], U8, name="tab_s")
+        nc.vector.memset(tab_s[:].bitcast(I32), 0)
+        w_s = keep.tile([P, H], U8, name="w_s")
+        nc.vector.memset(w_s[:].bitcast(I32), 0)
+
+        def load_weight_scales(source, first):
+            for quad in range(QUADS):
+                nc.sync.dma_start(
+                    w_s[32 * quad + first : 32 * quad + first + 4, :].bitcast(I32),
+                    source[0, 4 * quad : 4 * quad + 4, :].bitcast(I32),
+                )
+
+        idx1 = load_list("idx1", offs)
+        w2_raw = keep.tile([P, 2 * H], U8, name="w2_raw")
+        nc.sync.dma_start(w2_raw[:].bitcast(I32), w2_words[0].bitcast(I32))
+        w4_raw = keep.tile([P, H], I32, name="w4_raw")
+        nc.sync.dma_start(w4_raw[:], w4_words[0].rearrange("p c i -> p (c i)").bitcast(I32))
+        tab_w = [load_table_words(0)]
+        for quad in range(QUADS):
+            nc.sync.dma_start(
+                tab_s[32 * quad : 32 * quad + 4 * PASSES, :].bitcast(I32),
+                tab_scales[:, 4 * quad : 4 * quad + 4, :].bitcast(I32),
+            )
+        w1_pass = [w1[a * P * PACK : (a + 1) * P * PACK, :] for a in range(PASSES)]
+        w1_raw = [load_weight_rows(w1_pass[0]), load_weight_rows(w1_pass[1])]
+        load_weight_scales(w2_scales, 0)
+        tab_w.append(load_table_words(1))
+        load_weight_scales(w4_scales, 4)
+        w1_raw.append(load_weight_rows(w1_pass[2]))
+        tab_w.append(load_table_words(2))
+        idx2 = load_list("idx2", offs2)
+        wgs_first = load_wgs("wgs_first", slice(0, 1), slice(0, BANK))
+        pages = [load_page(0)]
+        wgs_second = load_wgs("wgs_second", slice(0, 1), slice(BANK, S))
+        pages.append(load_page(1))
+        idx3 = load_list("idx3", offs3)
+        wgs_1 = load_wgs("wgs_1", slice(1, 2), slice(0, S))
+        wgs_23 = load_wgs("wgs_23", slice(2, 4), slice(0, S))
+        w3_raw = load_weight_rows(w3)
+        pages.append(load_page(2))
+        idx4 = load_list("idx4", offs4)
+        pages.append(load_page(3))
+
+        gain_t = load_vector("gain_t", gain)
+        wear_t = load_vector("wear_t", wear)
+        lift_t = load_vector("lift_t", lift)
+        octave_t = load_vector("octave_t", octave)
+
+        v_s = keep.tile([P, S], U8, name="v_s", align_bytes=64)
+        h_banks = [[bank(HALVES * t + half, [P, BANK]) for half in range(HALVES)] for t in range(PACK)]
+        h = [keep.tile([P, S], F32, name="h%d" % t, align_bytes=64) for t in range(PACK)]
+        w2_p = keep.tile([P, 2 * H], U8, name="w2_p", align_bytes=64)
+        w4_p = keep.tile([P, H], I32, name="w4_p", align_bytes=64)
+        w_sp = keep.tile([P, H], U8, name="w_sp", align_bytes=64)
+        nc.vector.tensor_copy(
+            w2_p[:].rearrange("p (t m b) -> p m t b", t=PACK, b=2),
+            w2_raw[:].rearrange("p (m t b) -> p m t b", t=PACK, b=2),
+        )
+        nc.vector.tensor_copy(
+            w4_p[:].rearrange("p (t m) -> p m t", t=PACK), w4_raw[:].rearrange("p (m t) -> p m t", t=PACK)
+        )
+        for a in range(PASSES):
+            v_w = keep.tile([P, S], U32, name="v_w%d" % a, align_bytes=64)
+            last = a == PASSES - 1
+            if last:
+                nc.vector.tensor_copy(v_w[:, 0:BANK], tab_w[a][:].indirect(idx1[:, 0 : BANK // 16]))
+                codes, scales = quantize_weight("w1_%d" % a, w1_raw[a])
+                nc.vector.tensor_copy(v_w[:, BANK:S], tab_w[a][:].indirect(idx1[:, BANK // 16 : S // 16]))
+            else:
+                nc.vector.tensor_copy(v_w[:], tab_w[a][:].indirect(idx1[:]))
+                if a == 0:
+                    nc.vector.tensor_copy(v_s[:], tab_s[:].indirect(idx1[:]))
+                codes, scales = quantize_weight("w1_%d" % a, w1_raw[a])
+            for t in range(PACK):
+                rows = slice(P * t, P * (t + 1))
+                for half in range(HALVES):
+                    cols = slice(BANK * half, BANK * (half + 1))
+                    nc.tensor.matmul_mx(
+                        out=h_banks[t][half][:],
+                        lhsT=codes[:, rows].bitcast(FP8X4), lhsT_scale=scales[:, rows],
+                        rhs=v_w[:, cols].bitcast(FP8X4), rhs_scale=v_s[4 * a : P, cols],
+                        start=(a == 0), stop=last,
+                    )
+                    if last:
+                        nc.scalar.activation(h[t][:, cols], h_banks[t][half][:], COPY, scale=gain_t[:, t : t + 1])
+            if a == 1:
+                nc.vector.tensor_copy(
+                    w_sp[:].rearrange("p (t m) -> p m t", t=PACK), w_s[:].rearrange("p (m t) -> p m t", t=PACK)
+                )
+
+        x_tags = ["xk0", "xk1", "x2", "x3"]
+        x_grouped = [
+            keep.tile([P, CHUNK * PACK], BF16, name="x_grouped%d" % c, tag=x_tags[c], align_bytes=64)
+            for c in range(CHUNKS)
+        ]
+        chunk_list = [slice(c * CHUNK // 16, (c + 1) * CHUNK // 16) for c in range(CHUNKS)]
+
+        def scale_x(t, c, picked):
+            nc.scalar.activation(
+                x_grouped[c][:].rearrange("p (j t) -> p j t", t=PACK)[:, :, t],
+                picked[:, c * CHUNK : (c + 1) * CHUNK], COPY, scale=wear_t[:, t : t + 1],
+            )
+
+        for t in range(PACK):
+            if t == 0:
+                for half, factor in enumerate((wgs_first, wgs_second)):
+                    nc.vector.tensor_tensor(
+                        pages[t][:].indirect(idx2[:, half * BANK // 16 : (half + 1) * BANK // 16]),
+                        h[t][:, half * BANK : (half + 1) * BANK], factor[:, 0, :], MULT,
+                    )
+            else:
+                factor = wgs_1[:, 0, :] if t == 1 else wgs_23[:, t - 2, :]
+                nc.vector.tensor_tensor(pages[t][:].indirect(idx2[:]), h[t][:], factor, MULT)
+            picked = ring.tile([P, NP], F32, name="picked")
+            if t < PACK - 1:
+                nc.vector.tensor_copy(picked[:], pages[t][:].indirect(idx3[:]))
+                for c in range(CHUNKS):
+                    scale_x(t, c, picked)
+            else:
+                for c in range(CHUNKS):
+                    nc.vector.tensor_copy(
+                        picked[:, c * CHUNK : (c + 1) * CHUNK], pages[t][:].indirect(idx3[:, chunk_list[c]])
+                    )
+                    scale_x(t, c, picked)
+            if t == 2:
+                w3_codes, w3_scales = quantize_weight("w3", w3_raw, "h2")
+
+        out_rows = out.rearrange("(p t) j -> p t j", t=PACK)
+        key_tags = ["xk0", "xk1", "gk0", "gk1"]
+        g_tags = ["gk0", "gk1", "g2", "g3"]
+        keys = {}
+        g_mx = {}
+
+        def pick_keys(c):
+            keys[c] = keep.tile([P, PACK, CHUNK], F32, name="keys%d" % c, tag=key_tags[c], align_bytes=64)
+            for t in range(PACK):
+                nc.vector.tensor_copy(keys[c][:, t, :], pages[t][:].indirect(idx4[:, chunk_list[c]]))
+
+        def stage2(c, x_codes, x_scales):
+            last = c == CHUNKS - 1
+            th = ring.tile([P, PACK * CHUNK], F32, name="th")
+            for part in range(CHUNK // P):
+                cols = slice(part * P, (part + 1) * P)
+                z = bank(2 * (c % 2) + part, [P, PACK, P])
+                for t in range(PACK):
+                    nc.tensor.matmul_mx(
+                        out=z[:, t, :],
+                        lhsT=w2_p[:, 2 * P * t : 2 * P * (t + 1)].bitcast(FP4X4),
+                        lhsT_scale=w_sp[:, P * t : P * (t + 1)],
+                        rhs=x_codes[:, cols].bitcast(FP8X4), rhs_scale=x_scales[:, cols],
+                        start=True, stop=True,
+                    )
+                if last:
+                    nc.scalar.activation(
+                        th[:].rearrange("p (j t) -> p j t", t=PACK)[:, cols, :],
+                        z[:].rearrange("p t j -> p j t"), TANH,
+                    )
+                else:
+                    nc.scalar.activation(th[:].rearrange("p (t j) -> p t j", t=PACK)[:, :, cols], z[:], TANH)
+            g_grouped = keep.tile([P, CHUNK * PACK], BF16, name="g_grouped%d" % c, tag=g_tags[c], align_bytes=64)
+            if last:
+                nc.vector.tensor_tensor(
+                    g_grouped[:].rearrange("p (j t) -> p j t", t=PACK),
+                    th[:].rearrange("p (j t) -> p j t", t=PACK),
+                    lift_t[:].unsqueeze(1).to_broadcast([P, CHUNK, PACK]), MULT,
+                )
+            else:
+                g_planes = ring.tile([P, PACK, CHUNK], BF16, name="g_planes")
+                for t in range(PACK):
+                    nc.scalar.activation(
+                        g_planes[:, t, :], th[:, t * CHUNK : (t + 1) * CHUNK], COPY, scale=lift_t[:, t : t + 1]
+                    )
+                nc.scalar.copy(
+                    out=g_grouped[:].rearrange("p (c i t) -> p c t i", i=4, t=PACK),
+                    in_=g_planes[:].rearrange("p t (c i) -> p c t i", i=4),
+                )
+            g_mx[c] = quantize("g%d" % c, g_grouped, CHUNK)
+
+        def stage3(c):
+            g_codes, g_scales = g_mx[c]
+            y = [bank(4 + b, [P, 2, CHUNK]) for b in range(2)]
+            y2 = [bank(6 + b, [P, 2, CHUNK]) for b in range(2)]
+            for t in range(PACK):
+                rows = slice(P * t, P * (t + 1))
+                nc.tensor.matmul_mx(
+                    out=y[t // 2][:, t % 2, :], lhsT=w3_codes[:, rows].bitcast(FP8X4), lhsT_scale=w3_scales[:, rows],
+                    rhs=g_codes[:].bitcast(FP8X4), rhs_scale=g_scales[:], start=True, stop=True,
+                )
+            for t in range(PACK):
+                rows = slice(P * t, P * (t + 1))
+                nc.tensor.matmul_mx(
+                    out=y2[t // 2][:, t % 2, :], lhsT=w4_p[:, rows].bitcast(FP8X4), lhsT_scale=w_sp[4:P, rows],
+                    rhs=g_codes[:].bitcast(FP8X4), rhs_scale=g_scales[:], start=True, stop=True,
+                )
+            prod = ring.tile([P, PACK, CHUNK], F32, name="prod")
+            for t in range(PACK):
+                nc.vector.scalar_tensor_tensor(
+                    prod[:, t, :], y[t // 2][:, t % 2, :], octave_t[:, t : t + 1], keys[c][:, t, :], MULT, MULT
+                )
+            result = ring.tile([P, PACK, CHUNK], F32, name="result")
+            for b in range(2):
+                pair = slice(2 * b, 2 * b + 2)
+                nc.vector.tensor_tensor(result[:, pair, :], y2[b][:], prod[:, pair, :], ADD)
+                nc.sync.dma_start(out_rows[:, pair, c * CHUNK : (c + 1) * CHUNK], result[:, pair, :])
+
+        x_mx = {}
+        for c in range(CHUNKS):
+            x_mx[c] = quantize("x%d" % c, x_grouped[c], CHUNK)
+            if c < 2:
+                pick_keys(c)
+        for c in range(CHUNKS):
+            stage2(c, *x_mx[c])
+            if c < 2:
+                pick_keys(c + 2)
+            if 1 <= c + 1 < CHUNKS - 1:
+                stage3(c)
+        for c in range(CHUNKS - 2, CHUNKS):
+            stage3(c)

@@ -107,13 +107,14 @@ def tile_list_key_action_ledger_kernel(
         w4_raw = keep.tile([P, H], I32, name="w4_raw")
         nc.sync.dma_start(w4_raw[:], w4_words[0].rearrange("p c i -> p (c i)").bitcast(I32))
         tab_w = [load_table_words(0)]
+        w1_pass = [w1[a * P * PACK : (a + 1) * P * PACK, :] for a in range(PASSES)]
+        w1_raw = [load_weight_rows(w1_pass[0])]
         for quad in range(QUADS):
             nc.sync.dma_start(
                 tab_s[32 * quad : 32 * quad + 4 * PASSES, :].bitcast(I32),
                 tab_scales[:, 4 * quad : 4 * quad + 4, :].bitcast(I32),
             )
-        w1_pass = [w1[a * P * PACK : (a + 1) * P * PACK, :] for a in range(PASSES)]
-        w1_raw = [load_weight_rows(w1_pass[0]), load_weight_rows(w1_pass[1])]
+        w1_raw.append(load_weight_rows(w1_pass[1]))
         load_weight_scales(w2_scales, 0)
         tab_w.append(load_table_words(1))
         load_weight_scales(w4_scales, 4)
@@ -136,6 +137,10 @@ def tile_list_key_action_ledger_kernel(
         wear_t = load_vector("wear_t", wear)
         lift_t = load_vector("lift_t", lift)
         octave_t = load_vector("octave_t", octave)
+
+        warm = keep.tile([P, 2], F32, name="warm")
+        nc.gpsimd.memset(warm[:, 0:1], 0.0)
+        nc.scalar.activation(warm[:, 1:2], warm[:, 0:1], TANH)
 
         v_s = keep.tile([P, S], U8, name="v_s", align_bytes=64)
         h_banks = [[bank(HALVES * t + half, [P, BANK]) for half in range(HALVES)] for t in range(PACK)]
@@ -213,8 +218,6 @@ def tile_list_key_action_ledger_kernel(
                         picked[:, c * CHUNK : (c + 1) * CHUNK], pages[t][:].indirect(idx3[:, chunk_list[c]])
                     )
                     scale_x(t, c, picked)
-            if t == 2:
-                w3_codes, w3_scales = quantize_weight("w3", w3_raw, "h2")
 
         out_rows = out.rearrange("(p t) j -> p t j", t=PACK)
         key_tags = ["xk0", "xk1", "gk0", "gk1"]
@@ -228,43 +231,27 @@ def tile_list_key_action_ledger_kernel(
                 nc.vector.tensor_copy(keys[c][:, t, :], pages[t][:].indirect(idx4[:, chunk_list[c]]))
 
         def stage2(c, x_codes, x_scales):
-            last = c == CHUNKS - 1
-            th = ring.tile([P, PACK * CHUNK], F32, name="th")
-            for part in range(CHUNK // P):
-                cols = slice(part * P, (part + 1) * P)
-                z = bank(2 * (c % 2) + part, [P, PACK, P])
-                for t in range(PACK):
+            th = ring.tile([P, PACK, CHUNK], F32, name="th")
+            for b in range(2):
+                z = bank(2 * (c % 2) + b, [P, 2, CHUNK])
+                for u in range(2):
+                    t = 2 * b + u
                     nc.tensor.matmul_mx(
-                        out=z[:, t, :],
+                        out=z[:, u, :],
                         lhsT=w2_p[:, 2 * P * t : 2 * P * (t + 1)].bitcast(FP4X4),
                         lhsT_scale=w_sp[:, P * t : P * (t + 1)],
-                        rhs=x_codes[:, cols].bitcast(FP8X4), rhs_scale=x_scales[:, cols],
+                        rhs=x_codes[:].bitcast(FP8X4), rhs_scale=x_scales[:],
                         start=True, stop=True,
                     )
-                if last:
-                    nc.scalar.activation(
-                        th[:].rearrange("p (j t) -> p j t", t=PACK)[:, cols, :],
-                        z[:].rearrange("p t j -> p j t"), TANH,
-                    )
-                else:
-                    nc.scalar.activation(th[:].rearrange("p (t j) -> p t j", t=PACK)[:, :, cols], z[:], TANH)
+                nc.scalar.activation(th[:, 2 * b : 2 * b + 2, :], z[:], TANH)
             g_grouped = keep.tile([P, CHUNK * PACK], BF16, name="g_grouped%d" % c, tag=g_tags[c], align_bytes=64)
-            if last:
-                nc.vector.tensor_tensor(
-                    g_grouped[:].rearrange("p (j t) -> p j t", t=PACK),
-                    th[:].rearrange("p (j t) -> p j t", t=PACK),
-                    lift_t[:].unsqueeze(1).to_broadcast([P, CHUNK, PACK]), MULT,
-                )
-            else:
-                g_planes = ring.tile([P, PACK, CHUNK], BF16, name="g_planes")
-                for t in range(PACK):
-                    nc.scalar.activation(
-                        g_planes[:, t, :], th[:, t * CHUNK : (t + 1) * CHUNK], COPY, scale=lift_t[:, t : t + 1]
-                    )
-                nc.scalar.copy(
-                    out=g_grouped[:].rearrange("p (c i t) -> p c t i", i=4, t=PACK),
-                    in_=g_planes[:].rearrange("p t (c i) -> p c t i", i=4),
-                )
+            g_planes = ring.tile([P, PACK, CHUNK], BF16, name="g_planes")
+            for t in range(PACK):
+                nc.scalar.activation(g_planes[:, t, :], th[:, t, :], COPY, scale=lift_t[:, t : t + 1])
+            nc.scalar.copy(
+                out=g_grouped[:].rearrange("p (c i t) -> p c t i", i=4, t=PACK),
+                in_=g_planes[:].rearrange("p t (c i) -> p c t i", i=4),
+            )
             g_mx[c] = quantize("g%d" % c, g_grouped, CHUNK)
 
         def stage3(c):
@@ -283,12 +270,18 @@ def tile_list_key_action_ledger_kernel(
                     out=y2[t // 2][:, t % 2, :], lhsT=w4_p[:, rows].bitcast(FP8X4), lhsT_scale=w_sp[4:P, rows],
                     rhs=g_codes[:].bitcast(FP8X4), rhs_scale=g_scales[:], start=True, stop=True,
                 )
-            prod = ring.tile([P, PACK, CHUNK], F32, name="prod")
+            if c == 1:
+                prod = keep.tile([P, PACK, CHUNK], F32, name="prod1", tag="g2", align_bytes=64)
+            else:
+                prod = ring.tile([P, PACK, CHUNK], F32, name="prod")
             for t in range(PACK):
                 nc.vector.scalar_tensor_tensor(
                     prod[:, t, :], y[t // 2][:, t % 2, :], octave_t[:, t : t + 1], keys[c][:, t, :], MULT, MULT
                 )
-            result = ring.tile([P, PACK, CHUNK], F32, name="result")
+            if c == 2:
+                result = keep.tile([P, PACK, CHUNK], F32, name="result2", tag="g3", align_bytes=64)
+            else:
+                result = ring.tile([P, PACK, CHUNK], F32, name="result")
             for b in range(2):
                 pair = slice(2 * b, 2 * b + 2)
                 nc.vector.tensor_tensor(result[:, pair, :], y2[b][:], prod[:, pair, :], ADD)
@@ -299,11 +292,13 @@ def tile_list_key_action_ledger_kernel(
             x_mx[c] = quantize("x%d" % c, x_grouped[c], CHUNK)
             if c < 2:
                 pick_keys(c)
+        w3_codes, w3_scales = quantize_weight("w3", w3_raw, "h3")
         for c in range(CHUNKS):
             stage2(c, *x_mx[c])
             if c < 2:
                 pick_keys(c + 2)
-            if 1 <= c + 1 < CHUNKS - 1:
-                stage3(c)
-        for c in range(CHUNKS - 2, CHUNKS):
-            stage3(c)
+            if c == 0:
+                stage3(0)
+            if c >= 2:
+                stage3(c - 1)
+        stage3(CHUNKS - 1)

@@ -62,7 +62,7 @@ def tile_list_key_action_ledger_kernel(
         wgs_rows = wgs.rearrange("(q t) c -> q t c", t=PACK)
 
         def load_wgs(name, ts, cols):
-            tile = keep.tile([P, ts.stop - ts.start, cols.stop - cols.start], F32, name=name)
+            tile = keep.tile([P, ts.stop - ts.start, cols.stop - cols.start], F32, name=name, align_bytes=64)
             for quad in (0, 2, 1, 3):
                 nc.sync.dma_start(tile[32 * quad : 32 * quad + 32, :, :], wgs_rows[:, ts, cols])
             return tile
@@ -81,8 +81,8 @@ def tile_list_key_action_ledger_kernel(
         def quantize_weight(name, raw, tag=""):
             grouped = ring.tile([P, H * PACK], BF16, name="w_grouped", align_bytes=64)
             nc.scalar.copy(
-                out=grouped[:].rearrange("p (t m j) -> p m j t", t=PACK, j=PACK),
-                in_=raw[:].rearrange("p j (m t) -> p m j t", t=PACK),
+                out=grouped[:].rearrange("p (t m j) -> p m t j", t=PACK, j=PACK),
+                in_=raw[:].rearrange("p j (m t) -> p m t j", t=PACK),
             )
             return quantize(name, grouped, H, tag)
 
@@ -149,40 +149,58 @@ def tile_list_key_action_ledger_kernel(
         w4_p = keep.tile([P, H], I32, name="w4_p", align_bytes=64)
         w_sp = keep.tile([P, H], U8, name="w_sp", align_bytes=64)
         nc.vector.tensor_copy(
-            w2_p[:].rearrange("p (t m b) -> p m t b", t=PACK, b=2),
-            w2_raw[:].rearrange("p (m t b) -> p m t b", t=PACK, b=2),
+            w2_p[:].rearrange("p (t m b) -> p t m b", t=PACK, b=2),
+            w2_raw[:].rearrange("p (m t b) -> p t m b", t=PACK, b=2),
         )
         nc.vector.tensor_copy(
-            w4_p[:].rearrange("p (t m) -> p m t", t=PACK), w4_raw[:].rearrange("p (m t) -> p m t", t=PACK)
+            w4_p[:].rearrange("p (t m) -> p t m", t=PACK), w4_raw[:].rearrange("p (m t) -> p t m", t=PACK)
         )
-        for a in range(PASSES):
-            v_w = keep.tile([P, S], U32, name="v_w%d" % a, align_bytes=64)
+        def stage1_pass(a, t, v_w, codes, scales, rows):
             last = a == PASSES - 1
-            if last:
-                nc.vector.tensor_copy(v_w[:, 0:BANK], tab_w[a][:].indirect(idx1[:, 0 : BANK // 16]))
-                codes, scales = quantize_weight("w1_%d" % a, w1_raw[a])
-                nc.vector.tensor_copy(v_w[:, BANK:S], tab_w[a][:].indirect(idx1[:, BANK // 16 : S // 16]))
-            else:
-                nc.vector.tensor_copy(v_w[:], tab_w[a][:].indirect(idx1[:]))
-                if a == 0:
-                    nc.vector.tensor_copy(v_s[:], tab_s[:].indirect(idx1[:]))
-                codes, scales = quantize_weight("w1_%d" % a, w1_raw[a])
-            for t in range(PACK):
-                rows = slice(P * t, P * (t + 1))
-                for half in range(HALVES):
-                    cols = slice(BANK * half, BANK * (half + 1))
-                    nc.tensor.matmul_mx(
-                        out=h_banks[t][half][:],
-                        lhsT=codes[:, rows].bitcast(FP8X4), lhsT_scale=scales[:, rows],
-                        rhs=v_w[:, cols].bitcast(FP8X4), rhs_scale=v_s[4 * a : P, cols],
-                        start=(a == 0), stop=last,
-                    )
-                    if last:
-                        nc.scalar.activation(h[t][:, cols], h_banks[t][half][:], COPY, scale=gain_t[:, t : t + 1])
-            if a == 1:
-                nc.vector.tensor_copy(
-                    w_sp[:].rearrange("p (t m) -> p m t", t=PACK), w_s[:].rearrange("p (m t) -> p m t", t=PACK)
+            for half in range(HALVES):
+                cols = slice(BANK * half, BANK * (half + 1))
+                nc.tensor.matmul_mx(
+                    out=h_banks[t][half][:],
+                    lhsT=codes[:, rows].bitcast(FP8X4), lhsT_scale=scales[:, rows],
+                    rhs=v_w[:, cols].bitcast(FP8X4), rhs_scale=v_s[4 * a : P, cols],
+                    start=(a == 0), stop=last,
                 )
+                if last:
+                    nc.scalar.activation(h[t][:, cols], h_banks[t][half][:], COPY, scale=gain_t[:, t : t + 1])
+
+        for a in range(PASSES - 1):
+            v_w = keep.tile([P, S], U32, name="v_w%d" % a, align_bytes=64)
+            nc.vector.tensor_copy(v_w[:], tab_w[a][:].indirect(idx1[:]))
+            if a == 0:
+                nc.vector.tensor_copy(v_s[:], tab_s[:].indirect(idx1[:]))
+            codes, scales = quantize_weight("w1_%d" % a, w1_raw[a])
+            for t in range(PACK):
+                stage1_pass(a, t, v_w, codes, scales, slice(P * t, P * (t + 1)))
+        nc.vector.tensor_copy(
+            w_sp[:].rearrange("p (t m) -> p t m", t=PACK), w_s[:].rearrange("p (m t) -> p t m", t=PACK)
+        )
+
+        a = PASSES - 1
+        v_w = keep.tile([P, S], U32, name="v_w%d" % a, align_bytes=64)
+        for half in range(HALVES):
+            nc.vector.tensor_copy(
+                v_w[:, half * BANK : (half + 1) * BANK],
+                tab_w[a][:].indirect(idx1[:, half * BANK // 16 : (half + 1) * BANK // 16]),
+            )
+
+        def last_pass(ts, tag):
+            count = ts.stop - ts.start
+            grouped = keep.tile([P, count * P * PACK], BF16, name="w1_last%d" % ts.start, align_bytes=64)
+            nc.scalar.copy(
+                out=grouped[:].rearrange("p (t m j) -> p m t j", t=count, j=PACK),
+                in_=w1_raw[a][:].rearrange("p j (m t) -> p m t j", t=PACK)[:, :, ts, :],
+            )
+            codes, scales = quantize("w1_last%d" % ts.start, grouped, count * P, tag)
+            for u in range(count):
+                stage1_pass(a, ts.start + u, v_w, codes, scales, slice(P * u, P * (u + 1)))
+
+        last_pass(slice(0, 1), "")
+        last_pass(slice(1, 2), "")
 
         x_tags = ["xk0", "xk1", "x2", "x3"]
         x_grouped = [
@@ -204,6 +222,8 @@ def tile_list_key_action_ledger_kernel(
                         pages[t][:].indirect(idx2[:, half * BANK // 16 : (half + 1) * BANK // 16]),
                         h[t][:, half * BANK : (half + 1) * BANK], factor[:, 0, :], MULT,
                     )
+                    if half == 0:
+                        last_pass(slice(2, 4), "wgs_first")
             else:
                 factor = wgs_1[:, 0, :] if t == 1 else wgs_23[:, t - 2, :]
                 nc.vector.tensor_tensor(pages[t][:].indirect(idx2[:]), h[t][:], factor, MULT)
@@ -249,8 +269,8 @@ def tile_list_key_action_ledger_kernel(
             for t in range(PACK):
                 nc.scalar.activation(g_planes[:, t, :], th[:, t, :], COPY, scale=lift_t[:, t : t + 1])
             nc.scalar.copy(
-                out=g_grouped[:].rearrange("p (c i t) -> p c t i", i=4, t=PACK),
-                in_=g_planes[:].rearrange("p t (c i) -> p c t i", i=4),
+                out=g_grouped[:].rearrange("p (c i t) -> p c t i", i=2, t=PACK),
+                in_=g_planes[:].rearrange("p t (c i) -> p c t i", i=2),
             )
             g_mx[c] = quantize("g%d" % c, g_grouped, CHUNK)
 

@@ -1,6 +1,7 @@
 from contextlib import ExitStack
 
 import concourse.mybir as mybir
+from concourse.masks import make_identity
 
 K, T, S, H, T2, NP = 1536, 2048, 1024, 512, 2048, 1024
 FLOPS = 2 * (K * H * S + 3 * H * H * NP)
@@ -44,55 +45,33 @@ def tile_list_key_action_ledger_kernel(
             nc.sync.dma_start(tile[:], source)
             return tile
 
-        def load_weight_rows(rows):
-            raw = keep.tile([P, PACK, H], F32, name="w_raw", bufs=PASSES)
-            nc.sync.dma_start(raw[:], rows.rearrange("(p j) c -> p j c", j=PACK))
+        def load_weight_rows(name, rows, cols, tag=""):
+            raw = keep.tile([P, PACK, cols.stop - cols.start], F32, name=name, tag=tag, align_bytes=64)
+            nc.sync.dma_start(raw[:], rows.rearrange("(p j) c -> p j c", j=PACK)[:, :, cols])
             return raw
 
+        def load_w1(first, count):
+            cols = slice(first * P, (first + count) * P)
+            return [
+                load_weight_rows("w1_raw%d_%d" % (first, a), w1[a * P * PACK : (a + 1) * P * PACK, :], cols)
+                for a in range(PASSES)
+            ]
+
         def load_table_words(a):
-            words = keep.tile([P, T], U32, name="tab_w%d" % a)
+            words = keep.tile([P, T], U32, name="tab_w%d" % a, align_bytes=64)
             nc.sync.dma_start(words[:].bitcast(I32), tab_words[a].rearrange("p t i -> p (t i)").bitcast(I32))
             return words
 
-        def load_page(t):
-            page = keep.tile([P, T2], F32, name="page%d" % t)
-            nc.sync.dma_start(page[:], page0.rearrange("(p t) c -> p t c", t=PACK)[:, t, :])
+        def load_page(b):
+            page = keep.tile([P, T2], F32, name="page%d" % b)
+            nc.sync.dma_start(page[:], page0[b * P : (b + 1) * P, :])
             return page
 
-        wgs_rows = wgs.rearrange("(q t) c -> q t c", t=PACK)
-
-        def load_wgs(name, ts, cols):
-            tile = keep.tile([P, ts.stop - ts.start, cols.stop - cols.start], F32, name=name, align_bytes=64)
-            for quad in (0, 2, 1, 3):
-                nc.sync.dma_start(tile[32 * quad : 32 * quad + 32, :, :], wgs_rows[:, ts, cols])
-            return tile
-
-        def load_vector(name, source):
+        def load_vector(name, source, pattern):
             tile = keep.tile([P, PACK], F32, name=name)
-            nc.gpsimd.dma_start(tile[:], source.rearrange("(p t) -> p t", t=PACK))
+            with nc.allow_non_contiguous_dma(reason="one value a partition and block"):
+                nc.gpsimd.dma_start(tile[:], source.rearrange(pattern, p=P))
             return tile
-
-        def quantize(name, grouped, width, tag=""):
-            codes = keep.tile([P, width], U32, name=name + "_codes", tag=tag, align_bytes=64)
-            scales = keep.tile([P, width], U8, name=name + "_scales", align_bytes=64)
-            nc.vector.quantize_mx(out=codes[:].bitcast(FP8X4), scales=scales[:], in_=grouped[:])
-            return codes, scales
-
-        def quantize_weight(name, raw, tag=""):
-            grouped = ring.tile([P, H * PACK], BF16, name="w_grouped", align_bytes=64)
-            nc.scalar.copy(
-                out=grouped[:].rearrange("p (t m j) -> p m t j", t=PACK, j=PACK),
-                in_=raw[:].rearrange("p j (m t) -> p m t j", t=PACK),
-            )
-            return quantize(name, grouped, H, tag)
-
-        def bank(b, shape):
-            return psum.tile(shape, F32, name="bank%d" % b)
-
-        tab_s = keep.tile([P, T], U8, name="tab_s")
-        nc.vector.memset(tab_s[:].bitcast(I32), 0)
-        w_s = keep.tile([P, H], U8, name="w_s")
-        nc.vector.memset(w_s[:].bitcast(I32), 0)
 
         def load_weight_scales(source, first):
             for quad in range(QUADS):
@@ -101,148 +80,181 @@ def tile_list_key_action_ledger_kernel(
                     source[0, 4 * quad : 4 * quad + 4, :].bitcast(I32),
                 )
 
+        def quantize(name, grouped, width, tag=""):
+            codes = keep.tile([P, width], U32, name=name + "_codes", tag=tag, align_bytes=64)
+            scales = keep.tile([P, width], U8, name=name + "_scales", align_bytes=64)
+            nc.vector.quantize_mx(out=codes[:].bitcast(FP8X4), scales=scales[:], in_=grouped)
+            return codes, scales
+
+        def round_weight(name, raw, tag=""):
+            grouped = keep.tile([P, raw.shape[2] * PACK], BF16, name=name + "_grouped", tag=tag, align_bytes=64)
+            nc.scalar.copy(
+                out=grouped[:].rearrange("p (c i j) -> p c j i", i=2, j=PACK),
+                in_=raw[:].rearrange("p j (c i) -> p c j i", i=2),
+            )
+            return grouped
+
+        def bank(b, shape, dtype=F32):
+            return psum.tile(shape, dtype, name="bank%d" % b)
+
+        tab_s = keep.tile([P, T], U8, name="tab_s")
+        nc.vector.memset(tab_s[:].bitcast(I32), 0)
+        w_s = keep.tile([P, H], U8, name="w_s", align_bytes=64)
+        nc.vector.memset(w_s[:].bitcast(I32), 0)
+
         idx1 = load_list("idx1", offs)
         w2_raw = keep.tile([P, 2 * H], U8, name="w2_raw")
         nc.sync.dma_start(w2_raw[:].bitcast(I32), w2_words[0].bitcast(I32))
-        w4_raw = keep.tile([P, H], I32, name="w4_raw")
-        nc.sync.dma_start(w4_raw[:], w4_words[0].rearrange("p c i -> p (c i)").bitcast(I32))
-        tab_w = [load_table_words(0)]
-        w1_pass = [w1[a * P * PACK : (a + 1) * P * PACK, :] for a in range(PASSES)]
-        w1_raw = [load_weight_rows(w1_pass[0])]
+        tab_w = [load_table_words(0), load_table_words(1)]
         for quad in range(QUADS):
             nc.sync.dma_start(
                 tab_s[32 * quad : 32 * quad + 4 * PASSES, :].bitcast(I32),
                 tab_scales[:, 4 * quad : 4 * quad + 4, :].bitcast(I32),
             )
-        w1_raw.append(load_weight_rows(w1_pass[1]))
-        load_weight_scales(w2_scales, 0)
-        tab_w.append(load_table_words(1))
-        load_weight_scales(w4_scales, 4)
-        w1_raw.append(load_weight_rows(w1_pass[2]))
+        w1_raw = {0: load_w1(0, 1)}
         tab_w.append(load_table_words(2))
         idx2 = load_list("idx2", offs2)
-        wgs_first = load_wgs("wgs_first", slice(0, 1), slice(0, BANK))
+        wgs_t = keep.tile([P, S], F32, name="wgs_t", align_bytes=64)
+        nc.sync.dma_start(wgs_t[:, 0:BANK], wgs[:, 0:BANK])
         pages = [load_page(0)]
-        wgs_second = load_wgs("wgs_second", slice(0, 1), slice(BANK, S))
-        pages.append(load_page(1))
+        nc.sync.dma_start(wgs_t[:, BANK:S], wgs[:, BANK:S])
+        w1_raw[1] = load_w1(1, 1)
         idx3 = load_list("idx3", offs3)
-        wgs_1 = load_wgs("wgs_1", slice(1, 2), slice(0, S))
-        wgs_23 = load_wgs("wgs_23", slice(2, 4), slice(0, S))
-        w3_raw = load_weight_rows(w3)
+        pages.append(load_page(1))
+        w1_raw[2] = load_w1(2, 2)
+        load_weight_scales(w2_scales, 0)
         pages.append(load_page(2))
+        load_weight_scales(w4_scales, 4)
         idx4 = load_list("idx4", offs4)
+        w3_raw = load_weight_rows("w3_raw", w3, slice(0, H), "tab_w0")
         pages.append(load_page(3))
+        w4_w = keep.tile([P, H], I32, name="w4_w", align_bytes=64)
+        nc.sync.dma_start(w4_w[:], w4_words[0].rearrange("p c i -> p (c i)").bitcast(I32))
 
-        gain_t = load_vector("gain_t", gain)
-        wear_t = load_vector("wear_t", wear)
-        lift_t = load_vector("lift_t", lift)
-        octave_t = load_vector("octave_t", octave)
+        ident_f32 = keep.tile([P, P], F32, name="ident_f32")
+        make_identity(nc, ident_f32[:])
+        ident_bf16 = keep.tile([P, P], BF16, name="ident_bf16")
+        make_identity(nc, ident_bf16[:])
+        gain_t = load_vector("gain_t", gain, "(b p) -> p b")
+        wear_t = load_vector("wear_t", wear, "(b p) -> p b")
+        lift_t = load_vector("lift_t", lift, "(p t) -> p t")
+        octave_t = load_vector("octave_t", octave, "(b p) -> p b")
 
-        warm = keep.tile([P, 2], F32, name="warm")
-        nc.gpsimd.memset(warm[:, 0:1], 0.0)
-        nc.scalar.activation(warm[:, 1:2], warm[:, 0:1], TANH)
+        warm = keep.tile([P, 1], F32, name="warm")
+        nc.scalar.activation(warm[:], ident_f32[:, 0:1], TANH)
 
-        v_s = keep.tile([P, S], U8, name="v_s", align_bytes=64)
-        h_banks = [[bank(HALVES * t + half, [P, BANK]) for half in range(HALVES)] for t in range(PACK)]
-        h = [keep.tile([P, S], F32, name="h%d" % t, align_bytes=64) for t in range(PACK)]
         w2_p = keep.tile([P, 2 * H], U8, name="w2_p", align_bytes=64)
-        w4_p = keep.tile([P, H], I32, name="w4_p", align_bytes=64)
-        w_sp = keep.tile([P, H], U8, name="w_sp", align_bytes=64)
         nc.vector.tensor_copy(
             w2_p[:].rearrange("p (t m b) -> p t m b", t=PACK, b=2),
             w2_raw[:].rearrange("p (m t b) -> p t m b", t=PACK, b=2),
         )
-        nc.vector.tensor_copy(
-            w4_p[:].rearrange("p (t m) -> p t m", t=PACK), w4_raw[:].rearrange("p (m t) -> p t m", t=PACK)
-        )
-        def stage1_pass(a, t, v_w, codes, scales, rows):
-            last = a == PASSES - 1
-            for half in range(HALVES):
-                cols = slice(BANK * half, BANK * (half + 1))
-                nc.tensor.matmul_mx(
-                    out=h_banks[t][half][:],
-                    lhsT=codes[:, rows].bitcast(FP8X4), lhsT_scale=scales[:, rows],
-                    rhs=v_w[:, cols].bitcast(FP8X4), rhs_scale=v_s[4 * a : P, cols],
-                    start=(a == 0), stop=last,
-                )
-                if last:
-                    nc.scalar.activation(h[t][:, cols], h_banks[t][half][:], COPY, scale=gain_t[:, t : t + 1])
-
+        v_w = [keep.tile([P, S], U32, name="v_w%d" % a, align_bytes=64) for a in range(PASSES)]
+        v_s = keep.tile([P, S], U8, name="v_s", align_bytes=64)
         for a in range(PASSES - 1):
-            v_w = keep.tile([P, S], U32, name="v_w%d" % a, align_bytes=64)
-            nc.vector.tensor_copy(v_w[:], tab_w[a][:].indirect(idx1[:]))
-            if a == 0:
-                nc.vector.tensor_copy(v_s[:], tab_s[:].indirect(idx1[:]))
-            codes, scales = quantize_weight("w1_%d" % a, w1_raw[a])
-            for t in range(PACK):
-                stage1_pass(a, t, v_w, codes, scales, slice(P * t, P * (t + 1)))
-        nc.vector.tensor_copy(
-            w_sp[:].rearrange("p (t m) -> p t m", t=PACK), w_s[:].rearrange("p (m t) -> p t m", t=PACK)
-        )
-
-        a = PASSES - 1
-        v_w = keep.tile([P, S], U32, name="v_w%d" % a, align_bytes=64)
+            nc.vector.tensor_copy(v_w[a][:], tab_w[a][:].indirect(idx1[:]))
+        nc.vector.tensor_copy(v_s[:], tab_s[:].indirect(idx1[:]))
         for half in range(HALVES):
             nc.vector.tensor_copy(
-                v_w[:, half * BANK : (half + 1) * BANK],
-                tab_w[a][:].indirect(idx1[:, half * BANK // 16 : (half + 1) * BANK // 16]),
+                v_w[-1][:, half * BANK : (half + 1) * BANK],
+                tab_w[-1][:].indirect(idx1[:, half * BANK // 16 : (half + 1) * BANK // 16]),
             )
 
-        def last_pass(ts, tag):
-            count = ts.stop - ts.start
-            grouped = keep.tile([P, count * P * PACK], BF16, name="w1_last%d" % ts.start, align_bytes=64)
-            nc.scalar.copy(
-                out=grouped[:].rearrange("p (t m j) -> p m t j", t=count, j=PACK),
-                in_=w1_raw[a][:].rearrange("p j (m t) -> p m t j", t=PACK)[:, :, ts, :],
-            )
-            codes, scales = quantize("w1_last%d" % ts.start, grouped, count * P, tag)
+        h = {}
+
+        def stage1(first, count, grouped_tag, codes_tag):
+            grouped = [
+                round_weight("w1_%d_%d" % (first, a), w1_raw[first][a], grouped_tag if a == PASSES - 1 else "")
+                for a in range(PASSES)
+            ]
+            codes_tags = ["w1_raw%d_%d" % (first, PASSES - 1) if first else "", "", codes_tag]
+            w1_mx = [
+                quantize("w1_%d_%d" % (first, a), grouped[a][:], count * P, codes_tags[a]) for a in range(PASSES)
+            ]
             for u in range(count):
-                stage1_pass(a, ts.start + u, v_w, codes, scales, slice(P * u, P * (u + 1)))
+                b = first + u
+                rows = slice(P * u, P * (u + 1))
+                h[b] = keep.tile([P, S], F32, name="h%d" % b, align_bytes=64)
+                for half in range(HALVES):
+                    cols = slice(BANK * half, BANK * (half + 1))
+                    acc = bank(HALVES * (b % 2) + half, [P, BANK])
+                    for a in range(PASSES):
+                        codes, scales = w1_mx[a]
+                        nc.tensor.matmul_mx(
+                            out=acc[:],
+                            lhsT=codes[:, rows].bitcast(FP8X4), lhsT_scale=scales[:, rows],
+                            rhs=v_w[a][:, cols].bitcast(FP8X4), rhs_scale=v_s[4 * a : P, cols],
+                            start=(a == 0), stop=(a == PASSES - 1),
+                        )
+                    nc.scalar.activation(h[b][:, cols], acc[:], COPY, scale=gain_t[:, b : b + 1])
 
-        last_pass(slice(0, 1), "")
-        last_pass(slice(1, 2), "")
-
-        x_tags = ["xk0", "xk1", "x2", "x3"]
-        x_grouped = [
-            keep.tile([P, CHUNK * PACK], BF16, name="x_grouped%d" % c, tag=x_tags[c], align_bytes=64)
-            for c in range(CHUNKS)
-        ]
         chunk_list = [slice(c * CHUNK // 16, (c + 1) * CHUNK // 16) for c in range(CHUNKS)]
+        BLOCKS = CHUNK // P
+        x_turned = [keep.tile([P, BLOCKS, H], BF16, name="x_turned%d" % c) for c in range(CHUNKS)]
+        picked_tags = ["hold1", "hold2", "hold1", "hold2"]
 
-        def scale_x(t, c, picked):
-            nc.scalar.activation(
-                x_grouped[c][:].rearrange("p (j t) -> p j t", t=PACK)[:, :, t],
-                picked[:, c * CHUNK : (c + 1) * CHUNK], COPY, scale=wear_t[:, t : t + 1],
-            )
+        def turn_x(b, c, x_rows):
+            turned = bank(4 + c % 2, [P, BLOCKS, P], BF16)
+            for k in range(BLOCKS):
+                first = c * CHUNK + k * P
+                nc.tensor.transpose(turned[:, k, :], x_rows[:, first : first + P], ident_bf16[:])
+            nc.scalar.copy(out=x_turned[c][:, :, b * P : (b + 1) * P], in_=turned[:])
 
-        for t in range(PACK):
-            if t == 0:
-                for half, factor in enumerate((wgs_first, wgs_second)):
+        stage1(0, 1, "", "")
+        for b in range(PACK):
+            if b < PACK - 1:
+                for half in range(HALVES):
+                    cols = slice(half * BANK, (half + 1) * BANK)
                     nc.vector.tensor_tensor(
-                        pages[t][:].indirect(idx2[:, half * BANK // 16 : (half + 1) * BANK // 16]),
-                        h[t][:, half * BANK : (half + 1) * BANK], factor[:, 0, :], MULT,
+                        pages[b][:].indirect(idx2[:, half * BANK // 16 : (half + 1) * BANK // 16]),
+                        h[b][:, cols], wgs_t[:, cols], MULT,
                     )
-                    if half == 0:
-                        last_pass(slice(2, 4), "wgs_first")
             else:
-                factor = wgs_1[:, 0, :] if t == 1 else wgs_23[:, t - 2, :]
-                nc.vector.tensor_tensor(pages[t][:].indirect(idx2[:]), h[t][:], factor, MULT)
-            picked = ring.tile([P, NP], F32, name="picked")
-            if t < PACK - 1:
-                nc.vector.tensor_copy(picked[:], pages[t][:].indirect(idx3[:]))
+                nc.vector.tensor_tensor(pages[b][:].indirect(idx2[:]), h[b][:], wgs_t[:], MULT)
+            if b == 0:
+                stage1(1, 1, "hold1", "rows0")
+            if b == 1:
+                stage1(2, 2, "hold2", "rows1")
+            picked = keep.tile([P, NP], F32, name="picked%d" % b, tag=picked_tags[b], align_bytes=64)
+            x_rows = keep.tile([P, NP], BF16, name="x_rows%d" % b, tag="rows%d" % (b % 2), align_bytes=64)
+            if b < PACK - 1:
+                nc.vector.tensor_copy(picked[:], pages[b][:].indirect(idx3[:]))
+                nc.scalar.activation(x_rows[:], picked[:], COPY, scale=wear_t[:, b : b + 1])
                 for c in range(CHUNKS):
-                    scale_x(t, c, picked)
+                    turn_x(b, c, x_rows)
             else:
+                x_grouped = []
                 for c in range(CHUNKS):
-                    nc.vector.tensor_copy(
-                        picked[:, c * CHUNK : (c + 1) * CHUNK], pages[t][:].indirect(idx3[:, chunk_list[c]])
-                    )
-                    scale_x(t, c, picked)
+                    cols = slice(c * CHUNK, (c + 1) * CHUNK)
+                    if c == 0:
+                        head = keep.tile([P, CHUNK], F32, name="picked_head", align_bytes=64)
+                        part = head[:]
+                    else:
+                        part = picked[:, cols]
+                    nc.vector.tensor_copy(part, pages[b][:].indirect(idx3[:, chunk_list[c]]))
+                    nc.scalar.activation(x_rows[:, cols], part, COPY, scale=wear_t[:, b : b + 1])
+                    turn_x(b, c, x_rows)
+                    back = bank(6 + c % 2, [P, BLOCKS, 2, P])
+                    for k in range(BLOCKS):
+                        words = x_turned[c][:, k, :].bitcast(F32)
+                        for u in range(2):
+                            nc.tensor.transpose(back[:, k, u, :], words[:, u : H // 2 : 2], ident_f32[:])
+                    grouped = keep.tile([P, BLOCKS, P, 2], F32, name="x_grouped%d" % c, tag="x%d" % c, align_bytes=64)
+                    nc.scalar.copy(out=grouped[:], in_=back[:].rearrange("p k u j -> p k j u"))
+                    x_grouped.append(grouped)
+            if b == 2:
+                w_sp = keep.tile([P, H], U8, name="w_sp", tag="h2", align_bytes=64)
+                nc.vector.tensor_copy(
+                    w_sp[:].rearrange("p (t m) -> p t m", t=PACK), w_s[:].rearrange("p (m t) -> p t m", t=PACK)
+                )
 
-        out_rows = out.rearrange("(p t) j -> p t j", t=PACK)
-        key_tags = ["xk0", "xk1", "gk0", "gk1"]
-        g_tags = ["gk0", "gk1", "g2", "g3"]
+        out_rows = out.rearrange("(b p) j -> p b j", p=P)
+        key_tags = ["picked_head", "x0", "x2", "g0"]
+        pieces = [(0, 0, CHUNK), (1, 0, CHUNK), (2, 0, CHUNK), (3, 0, P), (3, P, P)]
+        z_banks = [(0, 1), (2, 3), (0, 1), (2,), (3,)]
+        y_banks = [(4, 5), (4, 5), (4, 5), (0,), (4,)]
+        y2_banks = [(6, 7), (6, 7), (6, 7), (1,), (6,)]
         keys = {}
+        x_mx = {}
         g_mx = {}
 
         def pick_keys(c):
@@ -250,75 +262,78 @@ def tile_list_key_action_ledger_kernel(
             for t in range(PACK):
                 nc.vector.tensor_copy(keys[c][:, t, :], pages[t][:].indirect(idx4[:, chunk_list[c]]))
 
-        def stage2(c, x_codes, x_scales):
-            th = ring.tile([P, PACK, CHUNK], F32, name="th")
-            for b in range(2):
-                z = bank(2 * (c % 2) + b, [P, 2, CHUNK])
-                for u in range(2):
-                    t = 2 * b + u
-                    nc.tensor.matmul_mx(
-                        out=z[:, u, :],
-                        lhsT=w2_p[:, 2 * P * t : 2 * P * (t + 1)].bitcast(FP4X4),
-                        lhsT_scale=w_sp[:, P * t : P * (t + 1)],
-                        rhs=x_codes[:].bitcast(FP8X4), rhs_scale=x_scales[:],
-                        start=True, stop=True,
-                    )
-                nc.scalar.activation(th[:, 2 * b : 2 * b + 2, :], z[:], TANH)
-            g_grouped = keep.tile([P, CHUNK * PACK], BF16, name="g_grouped%d" % c, tag=g_tags[c], align_bytes=64)
-            g_planes = ring.tile([P, PACK, CHUNK], BF16, name="g_planes")
+        def product(numbers, width, weights, rhs, rhs_scale):
+            per_bank = BANK // width
+            tiles = [bank(b, [P, per_bank, width]) for b in numbers]
+            for t in range(PACK):
+                lhsT, lhsT_scale = weights(t)
+                nc.tensor.matmul_mx(
+                    out=tiles[t // per_bank][:, t % per_bank, :], lhsT=lhsT, lhsT_scale=lhsT_scale,
+                    rhs=rhs.bitcast(FP8X4), rhs_scale=rhs_scale, start=True, stop=True,
+                )
+            return tiles
+
+        def w2_columns(t):
+            return w2_p[:, 2 * P * t : 2 * P * (t + 1)].bitcast(FP4X4), w_sp[:, P * t : P * (t + 1)]
+
+        def w3_columns(t):
+            return w3_codes[:, P * t : P * (t + 1)].bitcast(FP8X4), w3_scales[:, P * t : P * (t + 1)]
+
+        def w4_columns(t):
+            return w4_w[:, P * t : P * (t + 1)].bitcast(FP8X4), w_s[4:P, P * t : P * (t + 1)]
+
+        def stage2(i):
+            c, first, width = pieces[i]
+            per_bank = BANK // width
+            x_codes, x_scales = x_mx[c]
+            cols = slice(first, first + width)
+            z = product(z_banks[i], width, w2_columns, x_codes[:, cols], x_scales[:, cols])
+            th = ring.tile([P, PACK, width], F32, name="th")
+            for b in range(len(z)):
+                nc.scalar.activation(th[:, b * per_bank : (b + 1) * per_bank, :], z[b][:], TANH)
+            g_planes = ring.tile([P, PACK, width], BF16, name="g_planes")
             for t in range(PACK):
                 nc.scalar.activation(g_planes[:, t, :], th[:, t, :], COPY, scale=lift_t[:, t : t + 1])
+            g_grouped = keep.tile([P, width * PACK], BF16, name="g_grouped%d" % i, tag="g%d" % i, align_bytes=64)
             nc.scalar.copy(
                 out=g_grouped[:].rearrange("p (c i t) -> p c t i", i=2, t=PACK),
                 in_=g_planes[:].rearrange("p t (c i) -> p c t i", i=2),
             )
-            g_mx[c] = quantize("g%d" % c, g_grouped, CHUNK)
+            g_mx[i] = quantize("g%d" % i, g_grouped[:], width)
 
-        def stage3(c):
-            g_codes, g_scales = g_mx[c]
-            y = [bank(4 + b, [P, 2, CHUNK]) for b in range(2)]
-            y2 = [bank(6 + b, [P, 2, CHUNK]) for b in range(2)]
-            for t in range(PACK):
-                rows = slice(P * t, P * (t + 1))
-                nc.tensor.matmul_mx(
-                    out=y[t // 2][:, t % 2, :], lhsT=w3_codes[:, rows].bitcast(FP8X4), lhsT_scale=w3_scales[:, rows],
-                    rhs=g_codes[:].bitcast(FP8X4), rhs_scale=g_scales[:], start=True, stop=True,
-                )
-            for t in range(PACK):
-                rows = slice(P * t, P * (t + 1))
-                nc.tensor.matmul_mx(
-                    out=y2[t // 2][:, t % 2, :], lhsT=w4_p[:, rows].bitcast(FP8X4), lhsT_scale=w_sp[4:P, rows],
-                    rhs=g_codes[:].bitcast(FP8X4), rhs_scale=g_scales[:], start=True, stop=True,
-                )
-            if c == 1:
-                prod = keep.tile([P, PACK, CHUNK], F32, name="prod1", tag="g2", align_bytes=64)
-            else:
-                prod = ring.tile([P, PACK, CHUNK], F32, name="prod")
+        def stage3(i):
+            c, first, width = pieces[i]
+            per_bank = BANK // width
+            g_codes, g_scales = g_mx[i]
+            y = product(y_banks[i], width, w3_columns, g_codes[:], g_scales[:])
+            y2 = product(y2_banks[i], width, w4_columns, g_codes[:], g_scales[:])
+            prod = ring.tile([P, PACK, width], F32, name="prod")
             for t in range(PACK):
                 nc.vector.scalar_tensor_tensor(
-                    prod[:, t, :], y[t // 2][:, t % 2, :], octave_t[:, t : t + 1], keys[c][:, t, :], MULT, MULT
+                    prod[:, t, :], y[t // per_bank][:, t % per_bank, :], octave_t[:, t : t + 1],
+                    keys[c][:, t, first : first + width], MULT, MULT,
                 )
-            if c == 2:
-                result = keep.tile([P, PACK, CHUNK], F32, name="result2", tag="g3", align_bytes=64)
-            else:
-                result = ring.tile([P, PACK, CHUNK], F32, name="result")
-            for b in range(2):
-                pair = slice(2 * b, 2 * b + 2)
-                nc.vector.tensor_tensor(result[:, pair, :], y2[b][:], prod[:, pair, :], ADD)
-                nc.sync.dma_start(out_rows[:, pair, c * CHUNK : (c + 1) * CHUNK], result[:, pair, :])
+            result = keep.tile([P, PACK, width], F32, name="result%d" % i, tag="g%d" % (i + 1), align_bytes=64)
+            for u in range(0, PACK, 2):
+                pair = slice(u, u + 2)
+                nc.vector.tensor_tensor(
+                    result[:, pair, :], y2[u // per_bank][:, u % per_bank : u % per_bank + 2, :], prod[:, pair, :], ADD
+                )
+                cols = slice(c * CHUNK + first, c * CHUNK + first + width)
+                nc.sync.dma_start(out_rows[:, pair, cols], result[:, pair, :])
 
-        x_mx = {}
+        pick_keys(0)
         for c in range(CHUNKS):
-            x_mx[c] = quantize("x%d" % c, x_grouped[c], CHUNK)
-            if c < 2:
-                pick_keys(c)
-        w3_codes, w3_scales = quantize_weight("w3", w3_raw, "h3")
-        for c in range(CHUNKS):
-            stage2(c, *x_mx[c])
-            if c < 2:
-                pick_keys(c + 2)
+            x_mx[c] = quantize("x%d" % c, x_grouped[c][:].rearrange("p k j u -> p (k j u)").bitcast(BF16), CHUNK)
             if c == 0:
-                stage3(0)
-            if c >= 2:
-                stage3(c - 1)
-        stage3(CHUNKS - 1)
+                pick_keys(1)
+            if c == 2:
+                pick_keys(2)
+        w3_codes, w3_scales = quantize("w3", round_weight("w3", w3_raw)[:], H, "h3")
+        for i in range(len(pieces)):
+            stage2(i)
+            if i == 0:
+                pick_keys(3)
+            else:
+                stage3(i - 1)
+        stage3(len(pieces) - 1)

@@ -67,12 +67,6 @@ def tile_list_key_action_ledger_kernel(
             nc.sync.dma_start(page[:], page0[b * P : (b + 1) * P, :])
             return page
 
-        def load_vector(name, source, pattern):
-            tile = keep.tile([P, PACK], F32, name=name)
-            with nc.allow_non_contiguous_dma(reason="one value a partition and block"):
-                nc.gpsimd.dma_start(tile[:], source.rearrange(pattern, p=P))
-            return tile
-
         def load_weight_scales(source, first):
             for quad in range(QUADS):
                 nc.sync.dma_start(
@@ -102,6 +96,9 @@ def tile_list_key_action_ledger_kernel(
         w_s = keep.tile([P, H], U8, name="w_s", align_bytes=64)
         nc.vector.memset(w_s[:].bitcast(I32), 0)
 
+        factor_rows = keep.tile([P, P], F32, name="factor_rows")
+        nc.vector.memset(factor_rows[:], 0.0)
+
         idx1 = load_list("idx1", offs)
         w2_raw = keep.tile([P, 2 * H], U8, name="w2_raw")
         nc.sync.dma_start(w2_raw[:].bitcast(I32), w2_words[0].bitcast(I32))
@@ -112,6 +109,8 @@ def tile_list_key_action_ledger_kernel(
                 tab_scales[:, 4 * quad : 4 * quad + 4, :].bitcast(I32),
             )
         w1_raw = {0: load_w1(0, 1)}
+        for n, vector in enumerate((gain, wear, octave)):
+            nc.sync.dma_start(factor_rows[PACK * n : PACK * (n + 1), :], vector.rearrange("(b p) -> b p", p=P))
         tab_w.append(load_table_words(2))
         idx2 = load_list("idx2", offs2)
         wgs_t = keep.tile([P, S], F32, name="wgs_t", align_bytes=64)
@@ -126,6 +125,8 @@ def tile_list_key_action_ledger_kernel(
         pages.append(load_page(2))
         load_weight_scales(w4_scales, 4)
         idx4 = load_list("idx4", offs4)
+        lift_t = keep.tile([P, PACK], F32, name="lift_t")
+        nc.sync.dma_start(lift_t[:], lift.rearrange("(p t) -> p t", t=PACK))
         w3_raw = load_weight_rows("w3_raw", w3, slice(0, H), "tab_w0")
         pages.append(load_page(3))
         w4_w = keep.tile([P, H], I32, name="w4_w", align_bytes=64)
@@ -135,13 +136,15 @@ def tile_list_key_action_ledger_kernel(
         make_identity(nc, ident_f32[:])
         ident_bf16 = keep.tile([P, P], BF16, name="ident_bf16")
         make_identity(nc, ident_bf16[:])
-        gain_t = load_vector("gain_t", gain, "(b p) -> p b")
-        wear_t = load_vector("wear_t", wear, "(b p) -> p b")
-        lift_t = load_vector("lift_t", lift, "(p t) -> p t")
-        octave_t = load_vector("octave_t", octave, "(b p) -> p b")
 
         warm = keep.tile([P, 1], F32, name="warm")
         nc.scalar.activation(warm[:], ident_f32[:, 0:1], TANH)
+
+        factor_bank = bank(7, [P, P])
+        nc.tensor.transpose(factor_bank[:], factor_rows[:], ident_f32[:])
+        factors = keep.tile([P, 3, PACK], F32, name="factors")
+        nc.scalar.copy(out=factors[:].rearrange("p n b -> p (n b)"), in_=factor_bank[:, 0 : 3 * PACK])
+        gain_t, wear_t, octave_t = factors[:, 0, :], factors[:, 1, :], factors[:, 2, :]
 
         w2_p = keep.tile([P, 2 * H], U8, name="w2_p", align_bytes=64)
         nc.vector.tensor_copy(

from contextlib import ExitStack

import concourse.mybir as mybir
from concourse.masks import make_identity

K, T, S, H, T2, NP = 1536, 2048, 1024, 512, 2048, 1024
FLOPS = 2 * (K * H * S + 3 * H * H * NP)

F32 = mybir.dt.float32
BF16 = mybir.dt.bfloat16
I32 = mybir.dt.int32
U32 = mybir.dt.uint32
U16 = mybir.dt.uint16
U8 = mybir.dt.uint8
FP8X4 = mybir.dt.float8_e4m3fn_x4
FP4X4 = mybir.dt.float4_e2m1fn_x4
MULT = mybir.AluOpType.mult
ADD = mybir.AluOpType.add
COPY = mybir.ActivationFunctionType.Copy
TANH = mybir.ActivationFunctionType.Tanh

P = 128
PACK = 4
PASSES = K // (P * PACK)
BANK = 512
HALVES = S // BANK
CHUNK = 256
CHUNKS = NP // CHUNK
QUADS = 4


def tile_list_key_action_ledger_kernel(
    tc, tab_words, tab_scales, offs, offs2, offs3, offs4, w1, gain, wgs, page0, wear,
    w2_words, w2_scales, lift, w3, w4_words, w4_scales, octave, out,
):
    nc = tc.nc
    with ExitStack() as ctx:
        lists = ctx.enter_context(tc.tile_pool(name="lists", bufs=1))
        keep = ctx.enter_context(tc.tile_pool(name="keep", bufs=1))
        ring = ctx.enter_context(tc.tile_pool(name="ring", bufs=2))
        psum = ctx.enter_context(tc.psum_pool(name="psum", bufs=1))

        def load_list(name, source):
            tile = lists.tile([P, S // 16], U16, name=name)
            nc.sync.dma_start(tile[:], source)
            return tile

        def load_weight_rows(name, rows, cols, tag=""):
            raw = keep.tile([P, PACK, cols.stop - cols.start], F32, name=name, tag=tag, align_bytes=64)
            nc.sync.dma_start(raw[:], rows.rearrange("(p j) c -> p j c", j=PACK)[:, :, cols])
            return raw

        def load_w1(first, count):
            cols = slice(first * P, (first + count) * P)
            return [
                load_weight_rows("w1_raw%d_%d" % (first, a), w1[a * P * PACK : (a + 1) * P * PACK, :], cols)
                for a in range(PASSES)
            ]

        def load_table_words(a):
            words = keep.tile([P, T], U32, name="tab_w%d" % a, align_bytes=64)
            nc.sync.dma_start(words[:].bitcast(I32), tab_words[a].rearrange("p t i -> p (t i)").bitcast(I32))
            return words

        def load_page(b):
            page = keep.tile([P, T2], F32, name="page%d" % b)
            nc.sync.dma_start(page[:], page0[b * P : (b + 1) * P, :])
            return page

        def load_weight_scales(source, first):
            for quad in range(QUADS):
                nc.sync.dma_start(
                    w_s[32 * quad + first : 32 * quad + first + 4, :].bitcast(I32),
                    source[0, 4 * quad : 4 * quad + 4, :].bitcast(I32),
                )

        def quantize(name, grouped, width, tag=""):
            codes = keep.tile([P, width], U32, name=name + "_codes", tag=tag, align_bytes=64)
            scales = keep.tile([P, width], U8, name=name + "_scales", align_bytes=64)
            nc.vector.quantize_mx(out=codes[:].bitcast(FP8X4), scales=scales[:], in_=grouped)
            return codes, scales

        def round_weight(name, raw, tag=""):
            grouped = keep.tile([P, raw.shape[2] * PACK], BF16, name=name + "_grouped", tag=tag, align_bytes=64)
            nc.scalar.copy(
                out=grouped[:].rearrange("p (c i j) -> p c j i", i=2, j=PACK),
                in_=raw[:].rearrange("p j (c i) -> p c j i", i=2),
            )
            return grouped

        def bank(b, shape, dtype=F32):
            return psum.tile(shape, dtype, name="bank%d" % b)

        tab_s = keep.tile([P, T], U8, name="tab_s")
        nc.vector.memset(tab_s[:].bitcast(I32), 0)
        w_s = keep.tile([P, H], U8, name="w_s", align_bytes=64)
        nc.vector.memset(w_s[:].bitcast(I32), 0)

        factor_rows = keep.tile([P, P], F32, name="factor_rows")
        nc.vector.memset(factor_rows[:], 0.0)

        idx1 = load_list("idx1", offs)
        w2_raw = keep.tile([P, 2 * H], U8, name="w2_raw")
        nc.sync.dma_start(w2_raw[:].bitcast(I32), w2_words[0].bitcast(I32))
        tab_w = [load_table_words(0), load_table_words(1)]
        for quad in range(QUADS):
            nc.sync.dma_start(
                tab_s[32 * quad : 32 * quad + 4 * PASSES, :].bitcast(I32),
                tab_scales[:, 4 * quad : 4 * quad + 4, :].bitcast(I32),
            )
        w1_raw = {0: load_w1(0, 1)}
        for n, vector in enumerate((gain, wear, octave)):
            nc.sync.dma_start(factor_rows[PACK * n : PACK * (n + 1), :], vector.rearrange("(b p) -> b p", p=P))
        tab_w.append(load_table_words(2))
        idx2 = load_list("idx2", offs2)
        wgs_t = keep.tile([P, S], F32, name="wgs_t", align_bytes=64)
        nc.sync.dma_start(wgs_t[:, 0:BANK], wgs[:, 0:BANK])
        pages = [load_page(0)]
        nc.sync.dma_start(wgs_t[:, BANK:S], wgs[:, BANK:S])
        w1_raw[1] = load_w1(1, 1)
        idx3 = load_list("idx3", offs3)
        pages.append(load_page(1))
        w1_raw[2] = load_w1(2, 2)
        load_weight_scales(w2_scales, 0)
        pages.append(load_page(2))
        load_weight_scales(w4_scales, 4)
        idx4 = load_list("idx4", offs4)
        lift_t = keep.tile([P, PACK], F32, name="lift_t")
        nc.sync.dma_start(lift_t[:], lift.rearrange("(p t) -> p t", t=PACK))
        w3_raw = load_weight_rows("w3_raw", w3, slice(0, H), "tab_w0")
        pages.append(load_page(3))
        w4_w = keep.tile([P, H], I32, name="w4_w", align_bytes=64)
        nc.sync.dma_start(w4_w[:], w4_words[0].rearrange("p c i -> p (c i)").bitcast(I32))

        ident_f32 = keep.tile([P, P], F32, name="ident_f32")
        make_identity(nc, ident_f32[:])
        ident_bf16 = keep.tile([P, P], BF16, name="ident_bf16")
        make_identity(nc, ident_bf16[:])

        warm = keep.tile([P, 1], F32, name="warm")
        nc.scalar.activation(warm[:], ident_f32[:, 0:1], TANH)

        factor_bank = bank(7, [P, P])
        nc.tensor.transpose(factor_bank[:], factor_rows[:], ident_f32[:])
        factors = keep.tile([P, 3, PACK], F32, name="factors")
        nc.scalar.copy(out=factors[:].rearrange("p n b -> p (n b)"), in_=factor_bank[:, 0 : 3 * PACK])
        gain_t, wear_t, octave_t = factors[:, 0, :], factors[:, 1, :], factors[:, 2, :]

        w2_p = keep.tile([P, 2 * H], U8, name="w2_p", align_bytes=64)
        nc.vector.tensor_copy(
            w2_p[:].rearrange("p (t m b) -> p t m b", t=PACK, b=2),
            w2_raw[:].rearrange("p (m t b) -> p t m b", t=PACK, b=2),
        )
        v_w = [keep.tile([P, S], U32, name="v_w%d" % a, align_bytes=64) for a in range(PASSES)]
        v_s = keep.tile([P, S], U8, name="v_s", align_bytes=64)
        for a in range(PASSES - 1):
            nc.vector.tensor_copy(v_w[a][:], tab_w[a][:].indirect(idx1[:]))
        nc.vector.tensor_copy(v_s[:], tab_s[:].indirect(idx1[:]))
        for half in range(HALVES):
            nc.vector.tensor_copy(
                v_w[-1][:, half * BANK : (half + 1) * BANK],
                tab_w[-1][:].indirect(idx1[:, half * BANK // 16 : (half + 1) * BANK // 16]),
            )

        h = {}

        def stage1(first, count, grouped_tag, codes_tag):
            grouped = [
                round_weight("w1_%d_%d" % (first, a), w1_raw[first][a], grouped_tag if a == PASSES - 1 else "")
                for a in range(PASSES)
            ]
            codes_tags = ["w1_raw%d_%d" % (first, PASSES - 1) if first else "", "", codes_tag]
            w1_mx = [
                quantize("w1_%d_%d" % (first, a), grouped[a][:], count * P, codes_tags[a]) for a in range(PASSES)
            ]
            for u in range(count):
                b = first + u
                rows = slice(P * u, P * (u + 1))
                h[b] = keep.tile([P, S], F32, name="h%d" % b, align_bytes=64)
                for half in range(HALVES):
                    cols = slice(BANK * half, BANK * (half + 1))
                    acc = bank(HALVES * (b % 2) + half, [P, BANK])
                    for a in range(PASSES):
                        codes, scales = w1_mx[a]
                        nc.tensor.matmul_mx(
                            out=acc[:],
                            lhsT=codes[:, rows].bitcast(FP8X4), lhsT_scale=scales[:, rows],
                            rhs=v_w[a][:, cols].bitcast(FP8X4), rhs_scale=v_s[4 * a : P, cols],
                            start=(a == 0), stop=(a == PASSES - 1),
                        )
                    nc.scalar.activation(h[b][:, cols], acc[:], COPY, scale=gain_t[:, b : b + 1])

        chunk_list = [slice(c * CHUNK // 16, (c + 1) * CHUNK // 16) for c in range(CHUNKS)]
        BLOCKS = CHUNK // P
        x_turned = [keep.tile([P, BLOCKS, H], BF16, name="x_turned%d" % c) for c in range(CHUNKS)]
        picked_tags = ["hold1", "hold2", "hold1", "hold2"]

        def turn_x(b, c, x_rows):
            turned = bank(4 + c % 2, [P, BLOCKS, P], BF16)
            for k in range(BLOCKS):
                first = c * CHUNK + k * P
                nc.tensor.transpose(turned[:, k, :], x_rows[:, first : first + P], ident_bf16[:])
            nc.scalar.copy(out=x_turned[c][:, :, b * P : (b + 1) * P], in_=turned[:])

        stage1(0, 1, "", "")
        for b in range(PACK):
            if b < PACK - 1:
                for half in range(HALVES):
                    cols = slice(half * BANK, (half + 1) * BANK)
                    nc.vector.tensor_tensor(
                        pages[b][:].indirect(idx2[:, half * BANK // 16 : (half + 1) * BANK // 16]),
                        h[b][:, cols], wgs_t[:, cols], MULT,
                    )
            else:
                nc.vector.tensor_tensor(pages[b][:].indirect(idx2[:]), h[b][:], wgs_t[:], MULT)
            if b == 0:
                stage1(1, 1, "hold1", "rows0")
            if b == 1:
                stage1(2, 2, "hold2", "rows1")
            picked = keep.tile([P, NP], F32, name="picked%d" % b, tag=picked_tags[b], align_bytes=64)
            x_rows = keep.tile([P, NP], BF16, name="x_rows%d" % b, tag="rows%d" % (b % 2), align_bytes=64)
            if b < PACK - 1:
                nc.vector.tensor_copy(picked[:], pages[b][:].indirect(idx3[:]))
                nc.scalar.activation(x_rows[:], picked[:], COPY, scale=wear_t[:, b : b + 1])
                for c in range(CHUNKS):
                    turn_x(b, c, x_rows)
            else:
                x_grouped = []
                for c in range(CHUNKS):
                    cols = slice(c * CHUNK, (c + 1) * CHUNK)
                    if c == 0:
                        head = keep.tile([P, CHUNK], F32, name="picked_head", align_bytes=64)
                        part = head[:]
                    else:
                        part = picked[:, cols]
                    nc.vector.tensor_copy(part, pages[b][:].indirect(idx3[:, chunk_list[c]]))
                    nc.scalar.activation(x_rows[:, cols], part, COPY, scale=wear_t[:, b : b + 1])
                    turn_x(b, c, x_rows)
                    back = bank(6 + c % 2, [P, BLOCKS, 2, P])
                    for k in range(BLOCKS):
                        words = x_turned[c][:, k, :].bitcast(F32)
                        for u in range(2):
                            nc.tensor.transpose(back[:, k, u, :], words[:, u : H // 2 : 2], ident_f32[:])
                    grouped = keep.tile([P, BLOCKS, P, 2], F32, name="x_grouped%d" % c, tag="x%d" % c, align_bytes=64)
                    nc.scalar.copy(out=grouped[:], in_=back[:].rearrange("p k u j -> p k j u"))
                    x_grouped.append(grouped)
            if b == 2:
                w_sp = keep.tile([P, H], U8, name="w_sp", tag="h2", align_bytes=64)
                nc.vector.tensor_copy(
                    w_sp[:].rearrange("p (t m) -> p t m", t=PACK), w_s[:].rearrange("p (m t) -> p t m", t=PACK)
                )

        out_rows = out.rearrange("(b p) j -> p b j", p=P)
        key_tags = ["picked_head", "x0", "x2", "g0"]
        pieces = [(0, 0, CHUNK), (1, 0, CHUNK), (2, 0, CHUNK), (3, 0, P), (3, P, P)]
        z_banks = [(0, 1), (2, 3), (0, 1), (2,), (3,)]
        y_banks = [(4, 5), (4, 5), (4, 5), (0,), (4,)]
        y2_banks = [(6, 7), (6, 7), (6, 7), (1,), (6,)]
        keys = {}
        x_mx = {}
        g_mx = {}

        def pick_keys(c):
            keys[c] = keep.tile([P, PACK, CHUNK], F32, name="keys%d" % c, tag=key_tags[c], align_bytes=64)
            for t in range(PACK):
                nc.vector.tensor_copy(keys[c][:, t, :], pages[t][:].indirect(idx4[:, chunk_list[c]]))

        def product(numbers, width, weights, rhs, rhs_scale):
            per_bank = BANK // width
            tiles = [bank(b, [P, per_bank, width]) for b in numbers]
            for t in range(PACK):
                lhsT, lhsT_scale = weights(t)
                nc.tensor.matmul_mx(
                    out=tiles[t // per_bank][:, t % per_bank, :], lhsT=lhsT, lhsT_scale=lhsT_scale,
                    rhs=rhs.bitcast(FP8X4), rhs_scale=rhs_scale, start=True, stop=True,
                )
            return tiles

        def w2_columns(t):
            return w2_p[:, 2 * P * t : 2 * P * (t + 1)].bitcast(FP4X4), w_sp[:, P * t : P * (t + 1)]

        def w3_columns(t):
            return w3_codes[:, P * t : P * (t + 1)].bitcast(FP8X4), w3_scales[:, P * t : P * (t + 1)]

        def w4_columns(t):
            return w4_w[:, P * t : P * (t + 1)].bitcast(FP8X4), w_s[4:P, P * t : P * (t + 1)]

        def stage2(i):
            c, first, width = pieces[i]
            per_bank = BANK // width
            x_codes, x_scales = x_mx[c]
            cols = slice(first, first + width)
            z = product(z_banks[i], width, w2_columns, x_codes[:, cols], x_scales[:, cols])
            th = ring.tile([P, PACK, width], F32, name="th")
            for b in range(len(z)):
                nc.scalar.activation(th[:, b * per_bank : (b + 1) * per_bank, :], z[b][:], TANH)
            g_planes = ring.tile([P, PACK, width], BF16, name="g_planes")
            for t in range(PACK):
                nc.scalar.activation(g_planes[:, t, :], th[:, t, :], COPY, scale=lift_t[:, t : t + 1])
            g_grouped = keep.tile([P, width * PACK], BF16, name="g_grouped%d" % i, tag="g%d" % i, align_bytes=64)
            nc.scalar.copy(
                out=g_grouped[:].rearrange("p (c i t) -> p c t i", i=2, t=PACK),
                in_=g_planes[:].rearrange("p t (c i) -> p c t i", i=2),
            )
            g_mx[i] = quantize("g%d" % i, g_grouped[:], width)

        def stage3(i):
            c, first, width = pieces[i]
            per_bank = BANK // width
            g_codes, g_scales = g_mx[i]
            y = product(y_banks[i], width, w3_columns, g_codes[:], g_scales[:])
            y2 = product(y2_banks[i], width, w4_columns, g_codes[:], g_scales[:])
            prod = ring.tile([P, PACK, width], F32, name="prod")
            for t in range(PACK):
                nc.vector.scalar_tensor_tensor(
                    prod[:, t, :], y[t // per_bank][:, t % per_bank, :], octave_t[:, t : t + 1],
                    keys[c][:, t, first : first + width], MULT, MULT,
                )
            result = keep.tile([P, PACK, width], F32, name="result%d" % i, tag="g%d" % (i + 1), align_bytes=64)
            for u in range(0, PACK, 2):
                pair = slice(u, u + 2)
                nc.vector.tensor_tensor(
                    result[:, pair, :], y2[u // per_bank][:, u % per_bank : u % per_bank + 2, :], prod[:, pair, :], ADD
                )
                cols = slice(c * CHUNK + first, c * CHUNK + first + width)
                nc.sync.dma_start(out_rows[:, pair, cols], result[:, pair, :])

        pick_keys(0)
        for c in range(CHUNKS):
            x_mx[c] = quantize("x%d" % c, x_grouped[c][:].rearrange("p k j u -> p (k j u)").bitcast(BF16), CHUNK)
            if c == 0:
                pick_keys(1)
            if c == 2:
                pick_keys(2)
        w3_codes, w3_scales = quantize("w3", round_weight("w3", w3_raw)[:], H, "h3")
        for i in range(len(pieces)):
            stage2(i)
            if i == 0:
                pick_keys(3)
            else:
                stage3(i - 1)
        stage3(len(pieces) - 1)
